import numpy as np
import ml_dtypes


def mxq(x, axis, fmt="e4m3"):
    dtype, down = {"e4m3": (ml_dtypes.float8_e4m3fn, 7), "e5m2": (ml_dtypes.float8_e5m2, 14)}[fmt]
    v = np.moveaxis(np.asarray(x, np.float32).astype(ml_dtypes.bfloat16).astype(np.float64), axis, -1)
    blocks = v.reshape(v.shape[:-1] + (-1, 32))
    amax = np.abs(blocks).max(-1, keepdims=True)
    byte = np.maximum(np.where(amax > 0, np.frexp(amax)[1] - 1 + 127, 0) - down, 1)
    scale = np.exp2(byte - 127.0)
    codes = (blocks / scale).astype(np.float32).astype(dtype).astype(np.float64)
    return np.moveaxis((codes * scale).reshape(v.shape), -1, axis)


WIDE = False


def mx_kscale(k):
    if not WIDE:
        return np.ones(k)
    levels = np.array([10, -10, 5, -5, 0])
    if k % 512:
        return np.exp2(np.random.permutation(np.resize(levels, k // 32))).repeat(32)
    a = np.empty((k // 512, 16))
    for p in range(k // 512):
        a[p, :8] = np.random.permutation(np.resize(levels, 8))
        for g in range(8):
            far = levels[np.abs(levels - a[p, g]) >= 10]
            a[p, g + 8] = far[np.random.randint(len(far))]
    return np.exp2(a.ravel()).repeat(32)


def f64(x):
    return np.asarray(x).astype(np.float64)


def striped(idx):
    return np.tile(idx.reshape(-1, 16).T, (8, 1)).astype(np.uint16)


def unstriped(offs):
    return offs[:16].T.reshape(-1).astype(np.int64)


def pack_weight(w):
    k, n = w.shape
    w = f64(np.asarray(w, np.float32).astype(ml_dtypes.bfloat16)).reshape(k // 32, 32, n)
    amax = np.abs(w).max(1)
    byte = np.clip(np.where(amax > 0, np.frexp(amax)[1] - 1 + 127 - 7, 1), 1, 254)
    scaled = (w * np.exp2(127.0 - byte)[:, None, :]).reshape(k, n).astype(np.float32)
    words = np.ascontiguousarray(scaled.reshape(k // 512, 128, 4, n).transpose(0, 1, 3, 2)).astype(ml_dtypes.float8_e4m3fn).view(np.uint8)
    return words, np.ascontiguousarray(byte.astype(np.uint8).reshape(k // 512, 16, n))


def unpack_weight(words, scales):
    g, p, n, _ = words.shape
    vals = np.ascontiguousarray(words).view(ml_dtypes.float8_e4m3fn).astype(np.float64) * np.repeat(np.exp2(scales.astype(np.float64) - 127.0), 8, axis=1)[..., None]
    return vals.transpose(0, 1, 3, 2).reshape(g * 512, n)


def relu(v):
    return np.maximum(v, 0.0)


K, T, S, N, H, W = 512, 2048, 512, 256, 512, 2048


def setup_inputs():
    n = np.random.standard_normal
    s = mx_kscale(K)[:, None]
    u = mx_kscale(H)
    packed_xT = pack_weight(n((K, T)) * s)
    packed_eT = pack_weight(n((K, W)) * s)
    return {
        "x_words": packed_xT[0],
        "x_scales": packed_xT[1],
        "e_words": packed_eT[0],
        "e_scales": packed_eT[1],
        "w1": (n((K, H)) / np.sqrt(K) / s * u).astype(np.float32),
        "w2": (n((H, N)) / np.sqrt(H) / u[:, None]).astype(np.float32),
        "w3": (n((K, N)) / np.sqrt(K) / s).astype(np.float32),
        "bias": (0.5 * n((N, 1))).astype(np.float32),
        "offs": striped(np.random.permutation(T)[:S]),
        "fea": striped(np.random.permutation(W)[:S]),
    }


def reference(x_words, x_scales, e_words, e_scales, w1, w2, w3, bias, offs, fea):
    e_fea = unpack_weight(e_words, e_scales)[:, unstriped(fea)]
    fval = mxq(f64(w3), 0, "e4m3").T @ e_fea
    mu = fval.mean(axis=1, keepdims=True)
    dv = fval - mu
    dv2 = (dv) ** 2
    sd = np.sqrt(dv2.mean(axis=1, keepdims=True) + 0.05)
    xq = unpack_weight(x_words, x_scales)[:, unstriped(offs)]
    h = relu(mxq(f64(w1), 0, "e4m3").T @ xq)
    mask = mxq(f64(w2), 0, "e4m3").T @ mxq(h, 0, "e4m3")
    return relu((dv / sd) * mask + f64(bias))

@@ -1,0 +1,201 @@
+from contextlib import ExitStack
+
+import concourse.mybir as mybir
+
+K, T, S, N, H = 512, 2048, 512, 256, 512
+FLOPS = 2 * K * S * (H + N) + 2 * H * S * N
+
+F32 = mybir.dt.float32
+BF16 = mybir.dt.bfloat16
+U32 = mybir.dt.uint32
+I32 = mybir.dt.int32
+U16 = mybir.dt.uint16
+U8 = mybir.dt.uint8
+FP8X4 = mybir.dt.float8_e4m3fn_x4
+ACT = mybir.ActivationFunctionType
+ALU = mybir.AluOpType
+
+P = 128
+PACK = 4
+HALF = S // 2
+CHUNK = 128
+EPS = 0.05
+
+
+def tile_picked_ymaskn_relu_p_kernel(
+    tc, x_words, x_scales, e_words, e_scales, w1, w2, w3, bias, offs, fea, out
+):
+    nc = tc.nc
+    with ExitStack() as ctx:
+        keep = ctx.enter_context(tc.tile_pool(name="keep", bufs=1))
+        stage = ctx.enter_context(tc.tile_pool(name="stage", bufs=1))
+        psum = ctx.enter_context(tc.psum_pool(name="psum", bufs=1))
+
+        x_list = keep.tile([P, S // 16], U16, name="x_list")
+        e_list = keep.tile([P, S // 16], U16, name="e_list")
+        x_scale_tab = keep.tile([P, T], U8, name="x_scale_tab", align_bytes=64)
+        e_scale_tab = keep.tile([P, T], U8, name="e_scale_tab", align_bytes=64)
+        x_word_tab = stage.tile([P, T], U32, name="x_word_tab", tag="slot_c")
+
+        nc.vector.memset(x_scale_tab[:].bitcast(I32), 0)
+        nc.vector.memset(e_scale_tab[:].bitcast(I32), 0)
+
+        def load_scales(queue, tab, scales):
+            for r in range(4):
+                queue.dma_start(out=tab[r:P:32, :].bitcast(I32), in_=scales[0, r:16:4, :].bitcast(I32))
+
+        def load_words(tab, words):
+            nc.sync.dma_start(out=tab[:].bitcast(I32), in_=words[0].rearrange("p n t -> p (n t)").bitcast(I32))
+
+        def load_weight(w, c0, name, tag):
+            raw = stage.tile([P, PACK, 256], F32, name=name, tag=tag)
+            nc.sync.dma_start(out=raw[:], in_=w.rearrange("(p j) c -> p j c", j=PACK)[:, :, c0 : c0 + 256])
+            return raw
+
+        nc.sync.dma_start(x_list[:], offs)
+        nc.sync.dma_start(e_list[:], fea)
+        w1_raw = [load_weight(w1, 0, "w1_a", "slot_a"), load_weight(w1, 256, "w1_b", "slot_b")]
+        load_scales(nc.scalar, x_scale_tab, x_scales)
+        load_words(x_word_tab, x_words)
+        load_scales(nc.scalar, e_scale_tab, e_scales)
+        bias_sb = keep.tile([P, 2], F32, name="bias_sb")
+        with nc.allow_non_contiguous_dma(reason="one value a partition"):
+            nc.gpsimd.dma_start(out=bias_sb[:], in_=bias.rearrange("(m p) o -> p (m o)", p=P))
+        minus_half = keep.tile([P, 2], F32, name="minus_half")
+        nc.gpsimd.memset(minus_half[:], -0.5)
+
+        w1_bf = keep.tile([P, H * PACK], BF16, name="w1_bf", align_bytes=64)
+        w1_view = w1_bf[:].rearrange("p (t m j) -> p m t j", t=4, j=PACK)
+        for u in range(2):
+            nc.scalar.copy(
+                out=w1_view[:, 64 * u : 64 * u + 64],
+                in_=w1_raw[u][:].rearrange("p j (m t) -> p m t j", t=4),
+            )
+
+        w3_raw = load_weight(w3, 0, "w3_raw", "slot_a")
+        e_word_tab = stage.tile([P, T], U32, name="e_word_tab", tag="slot_b")
+        load_words(e_word_tab, e_words)
+
+        x_sc = keep.tile([P, S], U8, name="x_sc", align_bytes=64)
+        e_sc = keep.tile([P, S], U8, name="e_sc", align_bytes=64)
+        nc.vector.tensor_copy(x_sc[:], x_scale_tab[:].indirect(x_list[:]))
+
+        w1_q = keep.tile([P, H], U32, name="w1_q", align_bytes=64)
+        w1_s = keep.tile([P, H], U8, name="w1_s", align_bytes=64)
+        nc.vector.quantize_mx(out=w1_q[:].bitcast(FP8X4), scales=w1_s[:], in_=w1_bf[:])
+        nc.vector.tensor_copy(e_sc[:], e_scale_tab[:].indirect(e_list[:]))
+
+        def gather_words(tab, lst, u, name):
+            picked = keep.tile([P, HALF], U32, name=name, align_bytes=64)
+            nc.vector.tensor_copy(picked[:], tab[:].indirect(lst[:, 16 * u : 16 * u + 16]))
+            return picked
+
+        x_w = [gather_words(x_word_tab, x_list, u, f"x_w{u}") for u in range(2)]
+        w2_raw = load_weight(w2, 0, "w2_raw", "slot_c")
+
+        h_q = keep.tile([P, S], U32, name="h_q", align_bytes=64)
+        h_s = keep.tile([P, S], U8, name="h_s", align_bytes=64)
+        h_bf = []
+        for c in range(4):
+            bank = psum.tile([P, 4, CHUNK], F32, name=f"h_bank{c}")
+            for t in range(4):
+                nc.tensor.matmul_mx(
+                    out=bank[:, t, :],
+                    lhsT=w1_q[:, P * t : P * t + P].bitcast(FP8X4),
+                    lhsT_scale=w1_s[:, P * t : P * t + P],
+                    rhs=x_w[c // 2][:, CHUNK * (c % 2) : CHUNK * (c % 2) + CHUNK].bitcast(FP8X4),
+                    rhs_scale=x_sc[:, CHUNK * c : CHUNK * c + CHUNK],
+                    start=True,
+                    stop=True,
+                )
+            hb = keep.tile([P, CHUNK, PACK], BF16, name=f"h_bf{c}", align_bytes=64)
+            nc.scalar.activation(out=hb[:], in_=bank[:].rearrange("p t j -> p j t"), func=ACT.Relu)
+            h_bf.append(hb)
+
+        def weave(raw, bf, m):
+            src = raw[:, :, P * m : P * m + P].rearrange("p j (c i) -> p c j i", i=4)
+            dst = bf[:].rearrange("p (c i j) -> p c j i", i=4, j=PACK)
+            return dst, src
+
+        def quantised(bf, name):
+            q = keep.tile([P, P], U32, name=name + "_q", align_bytes=64)
+            s = keep.tile([P, P], U8, name=name + "_s", align_bytes=64)
+            nc.vector.quantize_mx(out=q[:].bitcast(FP8X4), scales=s[:], in_=bf[:])
+            return q, s
+
+        w3_bf = [keep.tile([P, P * PACK], BF16, name=f"w3_bf{m}", align_bytes=64) for m in range(2)]
+        for m in range(2):
+            dst, src = weave(w3_raw, w3_bf[m], m)
+            nc.vector.tensor_copy(dst, src)
+        w3_mx = [quantised(w3_bf[m], f"w3{m}") for m in range(2)]
+
+        for c in range(4):
+            nc.vector.quantize_mx(
+                out=h_q[:, CHUNK * c : CHUNK * c + CHUNK].bitcast(FP8X4),
+                scales=h_s[:, CHUNK * c : CHUNK * c + CHUNK],
+                in_=h_bf[c][:].rearrange("p j t -> p (j t)"),
+            )
+
+        e_w = [gather_words(e_word_tab, e_list, u, f"e_w{u}") for u in range(2)]
+        f_bank = [psum.tile([P, 2, HALF], F32, name=f"f_bank{u}") for u in range(2)]
+        for u in range(2):
+            for m in range(2):
+                nc.tensor.matmul_mx(
+                    out=f_bank[u][:, m, :],
+                    lhsT=w3_mx[m][0][:].bitcast(FP8X4),
+                    lhsT_scale=w3_mx[m][1][:],
+                    rhs=e_w[u][:].bitcast(FP8X4),
+                    rhs_scale=e_sc[:, HALF * u : HALF * u + HALF],
+                    start=True,
+                    stop=True,
+                )
+
+        w2_bf = [keep.tile([P, P * PACK], BF16, name=f"w2_bf{m}", align_bytes=64) for m in range(2)]
+        dst, src = weave(w2_raw, w2_bf[0], 0)
+        nc.scalar.copy(out=dst, in_=src)
+
+        stats = keep.tile([P, 2, 2, 6], F32, name="stats")
+        f_sb = [keep.tile([P, 2, HALF], F32, name=f"f_sb{u}") for u in range(2)]
+        for u in range(2):
+            for m in range(2):
+                nc.vector.bn_stats(out=stats[:, m, u, :], in_=f_bank[u][:, m, :])
+            nc.scalar.copy(out=f_sb[u][:], in_=f_bank[u][:])
+        mean_var = keep.tile([P, 2, 2], F32, name="mean_var")
+        for m in range(2):
+            nc.vector.bn_aggr(out=mean_var[:, m, :], in_=stats[:, m].rearrange("p u s -> p (u s)"))
+        var_eps = keep.tile([P, 2], F32, name="var_eps")
+        nc.gpsimd.tensor_scalar(var_eps[:], mean_var[:, :, 1], 1.0, EPS, ALU.mult, ALU.add)
+        rstd = keep.tile([P, 2], F32, name="rstd")
+        nc.gpsimd.tensor_tensor(rstd[:], var_eps[:], minus_half[:], ALU.pow)
+
+        w2_mx = [quantised(w2_bf[0], "w20")]
+        dst, src = weave(w2_raw, w2_bf[1], 1)
+        nc.vector.tensor_copy(dst, src)
+        w2_mx.append(quantised(w2_bf[1], "w21"))
+
+        for m in range(2):
+            mask = psum.tile([P, S], F32, name=f"mask{m}")
+            nc.tensor.matmul_mx(
+                out=mask[:],
+                lhsT=w2_mx[m][0][:].bitcast(FP8X4),
+                lhsT_scale=w2_mx[m][1][:],
+                rhs=h_q[:].bitcast(FP8X4),
+                rhs_scale=h_s[:],
+                start=True,
+                stop=True,
+            )
+            for u in range(2):
+                prod = keep.tile([P, HALF], F32, name=f"prod{m}{u}")
+                nc.vector.scalar_tensor_tensor(
+                    out=prod[:],
+                    in0=f_sb[u][:, m, :],
+                    scalar=mean_var[:, m, 0:1],
+                    in1=mask[:, HALF * u : HALF * u + HALF],
+                    op0=ALU.subtract,
+                    op1=ALU.mult,
+                )
+                res = keep.tile([P, HALF], F32, name=f"res{m}{u}")
+                nc.scalar.activation(
+                    out=res[:], in_=prod[:], func=ACT.Relu, scale=rstd[:, m : m + 1], bias=bias_sb[:, m : m + 1]
+                )
+                nc.sync.dma_start(out=out[P * m : P * m + P, HALF * u : HALF * u + HALF], in_=res[:])

@@ -28,41 +28,47 @@ def tile_picked_ymaskn_relu_p_kernel(
     nc = tc.nc
     with ExitStack() as ctx:
         keep = ctx.enter_context(tc.tile_pool(name="keep", bufs=1))
-        stage = ctx.enter_context(tc.tile_pool(name="stage", bufs=1))
         psum = ctx.enter_context(tc.psum_pool(name="psum", bufs=1))
 
         x_list = keep.tile([P, S // 16], U16, name="x_list")
         e_list = keep.tile([P, S // 16], U16, name="e_list")
         x_scale_tab = keep.tile([P, T], U8, name="x_scale_tab", align_bytes=64)
         e_scale_tab = keep.tile([P, T], U8, name="e_scale_tab", align_bytes=64)
-        x_word_tab = stage.tile([P, T], U32, name="x_word_tab", tag="slot_c")
+        x_word_tab = keep.tile([P, T], U32, name="x_word_tab")
+        e_word_tab = keep.tile([P, T], U32, name="e_word_tab", tag="e_word_slot", align_bytes=64)
 
         nc.vector.memset(x_scale_tab[:].bitcast(I32), 0)
         nc.vector.memset(e_scale_tab[:].bitcast(I32), 0)
 
-        def load_scales(queue, tab, scales):
+        def load_scales(tab, scales, first):
             for r in range(4):
-                queue.dma_start(out=tab[r:P:32, :].bitcast(I32), in_=scales[0, r:16:4, :].bitcast(I32))
+                nc.sync.dma_start(out=tab[first + r : P : 32, :].bitcast(I32), in_=scales[0, r:16:4, :].bitcast(I32))
 
         def load_words(tab, words):
             nc.sync.dma_start(out=tab[:].bitcast(I32), in_=words[0].rearrange("p n t -> p (n t)").bitcast(I32))
 
-        def load_weight(w, c0, name, tag):
-            raw = stage.tile([P, PACK, 256], F32, name=name, tag=tag)
+        def load_weight(w, c0, name):
+            raw = keep.tile([P, PACK, 256], F32, name=name)
             nc.sync.dma_start(out=raw[:], in_=w.rearrange("(p j) c -> p j c", j=PACK)[:, :, c0 : c0 + 256])
             return raw
 
         nc.sync.dma_start(x_list[:], offs)
-        nc.sync.dma_start(e_list[:], fea)
-        w1_raw = [load_weight(w1, 0, "w1_a", "slot_a"), load_weight(w1, 256, "w1_b", "slot_b")]
-        load_scales(nc.scalar, x_scale_tab, x_scales)
+        w1_raw = [load_weight(w1, 0, "w1_a")]
+        load_scales(x_scale_tab, x_scales, 0)
+        w1_raw.append(load_weight(w1, 256, "w1_b"))
         load_words(x_word_tab, x_words)
-        load_scales(nc.scalar, e_scale_tab, e_scales)
+        nc.sync.dma_start(e_list[:], fea)
+        load_scales(e_scale_tab, e_scales, 4)
+        w3_raw = load_weight(w3, 0, "w3_raw")
+        load_words(e_word_tab, e_words)
+        w2_raw = load_weight(w2, 0, "w2_raw")
         bias_sb = keep.tile([P, 2], F32, name="bias_sb")
         with nc.allow_non_contiguous_dma(reason="one value a partition"):
-            nc.gpsimd.dma_start(out=bias_sb[:], in_=bias.rearrange("(m p) o -> p (m o)", p=P))
-        minus_half = keep.tile([P, 2], F32, name="minus_half")
-        nc.gpsimd.memset(minus_half[:], -0.5)
+            nc.sync.dma_start(out=bias_sb[:], in_=bias.rearrange("(m p) o -> p (m o)", p=P))
+        one = keep.tile([P, 1], F32, name="one")
+        nc.gpsimd.memset(one[:], 1.0)
+        warm = keep.tile([P, 1], F32, name="warm")
+        nc.scalar.activation(out=warm[:], in_=one[:], func=ACT.Abs_reciprocal_sqrt)
 
         w1_bf = keep.tile([P, H * PACK], BF16, name="w1_bf", align_bytes=64)
         w1_view = w1_bf[:].rearrange("p (t m j) -> p m t j", t=4, j=PACK)
@@ -72,9 +78,6 @@ def tile_picked_ymaskn_relu_p_kernel(
                 in_=w1_raw[u][:].rearrange("p j (m t) -> p m t j", t=4),
             )
 
-        w3_raw = load_weight(w3, 0, "w3_raw", "slot_a")
-        e_word_tab = stage.tile([P, T], U32, name="e_word_tab", tag="slot_b")
-        load_words(e_word_tab, e_words)
 
         x_sc = keep.tile([P, S], U8, name="x_sc", align_bytes=64)
         e_sc = keep.tile([P, S], U8, name="e_sc", align_bytes=64)
@@ -83,7 +86,6 @@ def tile_picked_ymaskn_relu_p_kernel(
         w1_q = keep.tile([P, H], U32, name="w1_q", align_bytes=64)
         w1_s = keep.tile([P, H], U8, name="w1_s", align_bytes=64)
         nc.vector.quantize_mx(out=w1_q[:].bitcast(FP8X4), scales=w1_s[:], in_=w1_bf[:])
-        nc.vector.tensor_copy(e_sc[:], e_scale_tab[:].indirect(e_list[:]))
 
         def gather_words(tab, lst, u, name):
             picked = keep.tile([P, HALF], U32, name=name, align_bytes=64)
@@ -91,106 +93,97 @@ def tile_picked_ymaskn_relu_p_kernel(
             return picked
 
         x_w = [gather_words(x_word_tab, x_list, u, f"x_w{u}") for u in range(2)]
-        w2_raw = load_weight(w2, 0, "w2_raw", "slot_c")
+        nc.vector.tensor_copy(e_sc[:], e_scale_tab[:].indirect(e_list[:]))
 
-        h_q = keep.tile([P, S], U32, name="h_q", align_bytes=64)
-        h_s = keep.tile([P, S], U8, name="h_s", align_bytes=64)
-        h_bf = []
+        h_bf = [keep.tile([P, HALF, PACK], BF16, name=f"h_bf{u}", align_bytes=64) for u in range(2)]
         for c in range(4):
-            bank = psum.tile([P, 4, CHUNK], F32, name=f"h_bank{c}")
+            u, j0 = c // 2, CHUNK * (c % 2)
+            bank = psum.tile([P, 4, CHUNK], F32, name=f"h_bank{c}", tag=f"bank{c}")
             for t in range(4):
                 nc.tensor.matmul_mx(
                     out=bank[:, t, :],
                     lhsT=w1_q[:, P * t : P * t + P].bitcast(FP8X4),
                     lhsT_scale=w1_s[:, P * t : P * t + P],
-                    rhs=x_w[c // 2][:, CHUNK * (c % 2) : CHUNK * (c % 2) + CHUNK].bitcast(FP8X4),
+                    rhs=x_w[u][:, j0 : j0 + CHUNK].bitcast(FP8X4),
                     rhs_scale=x_sc[:, CHUNK * c : CHUNK * c + CHUNK],
                     start=True,
                     stop=True,
                 )
-            hb = keep.tile([P, CHUNK, PACK], BF16, name=f"h_bf{c}", align_bytes=64)
-            nc.scalar.activation(out=hb[:], in_=bank[:].rearrange("p t j -> p j t"), func=ACT.Relu)
-            h_bf.append(hb)
+            nc.scalar.activation(
+                out=h_bf[u][:, j0 : j0 + CHUNK, :], in_=bank[:].rearrange("p t j -> p j t"), func=ACT.Relu
+            )
 
-        def weave(raw, bf, m):
-            src = raw[:, :, P * m : P * m + P].rearrange("p j (c i) -> p c j i", i=4)
+        def weave(raw, bf, c0, width):
+            src = raw[:, :, c0 : c0 + width].rearrange("p j (c i) -> p c j i", i=4)
             dst = bf[:].rearrange("p (c i j) -> p c j i", i=4, j=PACK)
             return dst, src
 
-        def quantised(bf, name):
-            q = keep.tile([P, P], U32, name=name + "_q", align_bytes=64)
-            s = keep.tile([P, P], U8, name=name + "_s", align_bytes=64)
-            nc.vector.quantize_mx(out=q[:].bitcast(FP8X4), scales=s[:], in_=bf[:])
+        def quantised(bf, name, tag):
+            width = bf.shape[1] // PACK
+            q = keep.tile([P, width], U32, name=name + "_q", tag=tag, align_bytes=64)
+            s = keep.tile([P, width], U8, name=name + "_s", align_bytes=64)
+            nc.vector.quantize_mx(out=q[:].bitcast(FP8X4), scales=s[:], in_=bf)
             return q, s
 
-        w3_bf = [keep.tile([P, P * PACK], BF16, name=f"w3_bf{m}", align_bytes=64) for m in range(2)]
-        for m in range(2):
-            dst, src = weave(w3_raw, w3_bf[m], m)
-            nc.vector.tensor_copy(dst, src)
-        w3_mx = [quantised(w3_bf[m], f"w3{m}") for m in range(2)]
-
-        for c in range(4):
-            nc.vector.quantize_mx(
-                out=h_q[:, CHUNK * c : CHUNK * c + CHUNK].bitcast(FP8X4),
-                scales=h_s[:, CHUNK * c : CHUNK * c + CHUNK],
-                in_=h_bf[c][:].rearrange("p j t -> p (j t)"),
-            )
+        w3_bf = keep.tile([P, N * PACK], BF16, name="w3_bf", tag="w3_slot", align_bytes=64)
+        nc.vector.tensor_copy(*weave(w3_raw, w3_bf, 0, N))
+        w3_q, w3_s = quantised(w3_bf[:], "w3", "w3_q")
+        h_mx = [quantised(h_bf[0][:].rearrange("p j t -> p (j t)"), "h0", "w3_slot")]
 
         e_w = [gather_words(e_word_tab, e_list, u, f"e_w{u}") for u in range(2)]
+        h_mx.append(quantised(h_bf[1][:].rearrange("p j t -> p (j t)"), "h1", "e_word_slot"))
         f_bank = [psum.tile([P, 2, HALF], F32, name=f"f_bank{u}") for u in range(2)]
         for u in range(2):
             for m in range(2):
                 nc.tensor.matmul_mx(
                     out=f_bank[u][:, m, :],
-                    lhsT=w3_mx[m][0][:].bitcast(FP8X4),
-                    lhsT_scale=w3_mx[m][1][:],
+                    lhsT=w3_q[:, P * m : P * m + P].bitcast(FP8X4),
+                    lhsT_scale=w3_s[:, P * m : P * m + P],
                     rhs=e_w[u][:].bitcast(FP8X4),
-                    rhs_scale=e_sc[:, HALF * u : HALF * u + HALF],
+                    rhs_scale=e_sc[4:P, HALF * u : HALF * u + HALF],
                     start=True,
                     stop=True,
                 )
 
         w2_bf = [keep.tile([P, P * PACK], BF16, name=f"w2_bf{m}", align_bytes=64) for m in range(2)]
-        dst, src = weave(w2_raw, w2_bf[0], 0)
-        nc.scalar.copy(out=dst, in_=src)
+        for m in range(2):
+            nc.scalar.copy(*weave(w2_raw, w2_bf[m], P * m, P))
 
         stats = keep.tile([P, 2, 2, 6], F32, name="stats")
         f_sb = [keep.tile([P, 2, HALF], F32, name=f"f_sb{u}") for u in range(2)]
+        w2_mx = []
         for u in range(2):
             for m in range(2):
                 nc.vector.bn_stats(out=stats[:, m, u, :], in_=f_bank[u][:, m, :])
             nc.scalar.copy(out=f_sb[u][:], in_=f_bank[u][:])
+            w2_mx.append(quantised(w2_bf[u][:], f"w2{u}", f"w2{u}_q"))
         mean_var = keep.tile([P, 2, 2], F32, name="mean_var")
         for m in range(2):
             nc.vector.bn_aggr(out=mean_var[:, m, :], in_=stats[:, m].rearrange("p u s -> p (u s)"))
-        var_eps = keep.tile([P, 2], F32, name="var_eps")
-        nc.gpsimd.tensor_scalar(var_eps[:], mean_var[:, :, 1], 1.0, EPS, ALU.mult, ALU.add)
         rstd = keep.tile([P, 2], F32, name="rstd")
-        nc.gpsimd.tensor_tensor(rstd[:], var_eps[:], minus_half[:], ALU.pow)
+        nc.scalar.activation(out=rstd[:], in_=mean_var[:, :, 1], func=ACT.Abs_reciprocal_sqrt, bias=EPS)
 
-        w2_mx = [quantised(w2_bf[0], "w20")]
-        dst, src = weave(w2_raw, w2_bf[1], 1)
-        nc.vector.tensor_copy(dst, src)
-        w2_mx.append(quantised(w2_bf[1], "w21"))
-
+        mask = {}
         for m in range(2):
-            mask = psum.tile([P, S], F32, name=f"mask{m}")
-            nc.tensor.matmul_mx(
-                out=mask[:],
-                lhsT=w2_mx[m][0][:].bitcast(FP8X4),
-                lhsT_scale=w2_mx[m][1][:],
-                rhs=h_q[:].bitcast(FP8X4),
-                rhs_scale=h_s[:],
-                start=True,
-                stop=True,
-            )
+            for u in range(2):
+                mask[m, u] = psum.tile([P, HALF], F32, name=f"mask{m}{u}", tag=f"bank{2 * m + u}")
+                nc.tensor.matmul_mx(
+                    out=mask[m, u][:],
+                    lhsT=w2_mx[m][0][:].bitcast(FP8X4),
+                    lhsT_scale=w2_mx[m][1][:],
+                    rhs=h_mx[u][0][:].bitcast(FP8X4),
+                    rhs_scale=h_mx[u][1][:],
+                    start=True,
+                    stop=True,
+                )
+        for m in range(2):
             for u in range(2):
                 prod = keep.tile([P, HALF], F32, name=f"prod{m}{u}")
                 nc.vector.scalar_tensor_tensor(
                     out=prod[:],
                     in0=f_sb[u][:, m, :],
                     scalar=mean_var[:, m, 0:1],
-                    in1=mask[:, HALF * u : HALF * u + HALF],
+                    in1=mask[m, u][:],
                     op0=ALU.subtract,
                     op1=ALU.mult,
                 )

@@ -20,6 +20,7 @@ PACK = 4
 HALF = S // 2
 CHUNK = 128
 EPS = 0.05
+W1_SCALAR = 80
 
 
 def tile_picked_ymaskn_relu_p_kernel(
@@ -32,7 +33,7 @@ def tile_picked_ymaskn_relu_p_kernel(
 
         x_list = keep.tile([P, S // 16], U16, name="x_list")
         e_list = keep.tile([P, S // 16], U16, name="e_list")
-        x_scale_tab = keep.tile([P, T], U8, name="x_scale_tab", align_bytes=64)
+        x_scale_tab = keep.tile([P, T], U8, name="x_scale_tab", tag="x_scale_slot", align_bytes=64)
         e_scale_tab = keep.tile([P, T], U8, name="e_scale_tab", align_bytes=64)
         x_word_tab = keep.tile([P, T], U32, name="x_word_tab")
         e_word_tab = keep.tile([P, T], U32, name="e_word_tab", tag="e_word_slot", align_bytes=64)
@@ -47,21 +48,20 @@ def tile_picked_ymaskn_relu_p_kernel(
         def load_words(tab, words):
             nc.sync.dma_start(out=tab[:].bitcast(I32), in_=words[0].rearrange("p n t -> p (n t)").bitcast(I32))
 
-        def load_weight(w, c0, name):
-            raw = keep.tile([P, PACK, 256], F32, name=name)
-            nc.sync.dma_start(out=raw[:], in_=w.rearrange("(p j) c -> p j c", j=PACK)[:, :, c0 : c0 + 256])
+        def load_weight(w, name):
+            raw = keep.tile([P, PACK, w.shape[1]], F32, name=name, tag=name)
+            nc.sync.dma_start(out=raw[:], in_=w.rearrange("(p j) c -> p j c", j=PACK))
             return raw
 
         nc.sync.dma_start(x_list[:], offs)
-        w1_raw = [load_weight(w1, 0, "w1_a")]
+        w1_raw = load_weight(w1, "w1_raw")
         load_scales(x_scale_tab, x_scales, 0)
-        w1_raw.append(load_weight(w1, 256, "w1_b"))
         load_words(x_word_tab, x_words)
         nc.sync.dma_start(e_list[:], fea)
         load_scales(e_scale_tab, e_scales, 4)
-        w3_raw = load_weight(w3, 0, "w3_raw")
+        w3_raw = load_weight(w3, "w3_raw")
         load_words(e_word_tab, e_words)
-        w2_raw = load_weight(w2, 0, "w2_raw")
+        w2_raw = load_weight(w2, "w2_raw")
         bias_sb = keep.tile([P, 2], F32, name="bias_sb")
         with nc.allow_non_contiguous_dma(reason="one value a partition"):
             nc.sync.dma_start(out=bias_sb[:], in_=bias.rearrange("(m p) o -> p (m o)", p=P))
@@ -72,18 +72,16 @@ def tile_picked_ymaskn_relu_p_kernel(
 
         w1_bf = keep.tile([P, H * PACK], BF16, name="w1_bf", align_bytes=64)
         w1_view = w1_bf[:].rearrange("p (t m j) -> p m t j", t=4, j=PACK)
-        for u in range(2):
-            nc.scalar.copy(
-                out=w1_view[:, 64 * u : 64 * u + 64],
-                in_=w1_raw[u][:].rearrange("p j (m t) -> p m t j", t=4),
-            )
+        w1_src = w1_raw[:].rearrange("p j (m t) -> p m t j", t=4)
+        nc.scalar.copy(out=w1_view[:, :W1_SCALAR], in_=w1_src[:, :W1_SCALAR])
+        nc.vector.tensor_copy(out=w1_view[:, W1_SCALAR:], in_=w1_src[:, W1_SCALAR:])
 
 
         x_sc = keep.tile([P, S], U8, name="x_sc", align_bytes=64)
         e_sc = keep.tile([P, S], U8, name="e_sc", align_bytes=64)
         nc.vector.tensor_copy(x_sc[:], x_scale_tab[:].indirect(x_list[:]))
 
-        w1_q = keep.tile([P, H], U32, name="w1_q", align_bytes=64)
+        w1_q = keep.tile([P, H], U32, name="w1_q", tag="x_scale_slot", align_bytes=64)
         w1_s = keep.tile([P, H], U8, name="w1_s", align_bytes=64)
         nc.vector.quantize_mx(out=w1_q[:].bitcast(FP8X4), scales=w1_s[:], in_=w1_bf[:])
 
@@ -95,7 +93,7 @@ def tile_picked_ymaskn_relu_p_kernel(
         x_w = [gather_words(x_word_tab, x_list, u, f"x_w{u}") for u in range(2)]
         nc.vector.tensor_copy(e_sc[:], e_scale_tab[:].indirect(e_list[:]))
 
-        h_bf = [keep.tile([P, HALF, PACK], BF16, name=f"h_bf{u}", align_bytes=64) for u in range(2)]
+        h_bf = keep.tile([P, S * PACK], BF16, name="h_bf", align_bytes=64)
         for c in range(4):
             u, j0 = c // 2, CHUNK * (c % 2)
             bank = psum.tile([P, 4, CHUNK], F32, name=f"h_bank{c}", tag=f"bank{c}")
@@ -110,7 +108,9 @@ def tile_picked_ymaskn_relu_p_kernel(
                     stop=True,
                 )
             nc.scalar.activation(
-                out=h_bf[u][:, j0 : j0 + CHUNK, :], in_=bank[:].rearrange("p t j -> p j t"), func=ACT.Relu
+                out=h_bf[:, PACK * CHUNK * c : PACK * CHUNK * (c + 1)].rearrange("p (j t) -> p j t", t=PACK),
+                in_=bank[:].rearrange("p t j -> p j t"),
+                func=ACT.Relu,
             )
 
         def weave(raw, bf, c0, width):
@@ -125,18 +125,17 @@ def tile_picked_ymaskn_relu_p_kernel(
             nc.vector.quantize_mx(out=q[:].bitcast(FP8X4), scales=s[:], in_=bf)
             return q, s
 
-        w3_bf = keep.tile([P, N * PACK], BF16, name="w3_bf", tag="w3_slot", align_bytes=64)
+        w3_bf = keep.tile([P, N * PACK], BF16, name="w3_bf", align_bytes=64)
         nc.vector.tensor_copy(*weave(w3_raw, w3_bf, 0, N))
         w3_q, w3_s = quantised(w3_bf[:], "w3", "w3_q")
-        h_mx = [quantised(h_bf[0][:].rearrange("p j t -> p (j t)"), "h0", "w3_slot")]
 
         e_w = [gather_words(e_word_tab, e_list, u, f"e_w{u}") for u in range(2)]
-        h_mx.append(quantised(h_bf[1][:].rearrange("p j t -> p (j t)"), "h1", "e_word_slot"))
-        f_bank = [psum.tile([P, 2, HALF], F32, name=f"f_bank{u}") for u in range(2)]
+        h_q, h_s = quantised(h_bf[:], "h", "e_word_slot")
+        f_bank = [psum.tile([P, S], F32, name=f"f_bank{m}") for m in range(2)]
         for u in range(2):
             for m in range(2):
                 nc.tensor.matmul_mx(
-                    out=f_bank[u][:, m, :],
+                    out=f_bank[m][:, HALF * u : HALF * u + HALF],
                     lhsT=w3_q[:, P * m : P * m + P].bitcast(FP8X4),
                     lhsT_scale=w3_s[:, P * m : P * m + P],
                     rhs=e_w[u][:].bitcast(FP8X4),
@@ -145,50 +144,55 @@ def tile_picked_ymaskn_relu_p_kernel(
                     stop=True,
                 )
 
-        w2_bf = [keep.tile([P, P * PACK], BF16, name=f"w2_bf{m}", align_bytes=64) for m in range(2)]
+        w2_bf = [keep.tile([P, P * PACK], BF16, name=f"w2_bf{m}", tag=f"w2_slot{m}", align_bytes=64) for m in range(2)]
         for m in range(2):
             nc.scalar.copy(*weave(w2_raw, w2_bf[m], P * m, P))
 
-        stats = keep.tile([P, 2, 2, 6], F32, name="stats")
-        f_sb = [keep.tile([P, 2, HALF], F32, name=f"f_sb{u}") for u in range(2)]
-        w2_mx = []
-        for u in range(2):
-            for m in range(2):
-                nc.vector.bn_stats(out=stats[:, m, u, :], in_=f_bank[u][:, m, :])
-            nc.scalar.copy(out=f_sb[u][:], in_=f_bank[u][:])
-            w2_mx.append(quantised(w2_bf[u][:], f"w2{u}", f"w2{u}_q"))
-        mean_var = keep.tile([P, 2, 2], F32, name="mean_var")
-        for m in range(2):
-            nc.vector.bn_aggr(out=mean_var[:, m, :], in_=stats[:, m].rearrange("p u s -> p (u s)"))
-        rstd = keep.tile([P, 2], F32, name="rstd")
-        nc.scalar.activation(out=rstd[:], in_=mean_var[:, :, 1], func=ACT.Abs_reciprocal_sqrt, bias=EPS)
+        f_sb = keep.tile([P, 2, S], F32, name="f_sb", tag="w2_raw")
+        w2_mx = [quantised(w2_bf[m][:], f"w2{m}", f"w2{m}_q") for m in range(2)]
+        stats0 = keep.tile([P, 6], F32, name="stats0", tag="w2_slot0", align_bytes=64)
+        nc.vector.bn_stats(out=stats0[:], in_=f_bank[0][:])
+        nc.scalar.copy(out=f_sb[:, 0, :], in_=f_bank[0][:])
+        mean_var0 = keep.tile([P, 2], F32, name="mean_var0")
+        nc.vector.bn_aggr(out=mean_var0[:], in_=stats0[:])
+        stats1 = keep.tile([P, 6], F32, name="stats1", tag="w2_slot1", align_bytes=64)
+        nc.vector.bn_stats(out=stats1[:], in_=f_bank[1][:])
+        nc.scalar.copy(out=f_sb[:, 1, :], in_=f_bank[1][:])
+        mean_var1 = keep.tile([P, 2], F32, name="mean_var1")
+        nc.vector.bn_aggr(out=mean_var1[:], in_=stats1[:])
+        mean_var = [mean_var0, mean_var1]
 
-        mask = {}
         for m in range(2):
+            rstd = keep.tile([P, 1], F32, name=f"rstd{m}")
+            nc.scalar.activation(out=rstd[:], in_=mean_var[m][:, 1:2], func=ACT.Abs_reciprocal_sqrt, bias=EPS)
+            mask = []
             for u in range(2):
-                mask[m, u] = psum.tile([P, HALF], F32, name=f"mask{m}{u}", tag=f"bank{2 * m + u}")
+                mask.append(psum.tile([P, HALF], F32, name=f"mask{m}{u}", tag=f"bank{2 * m + u}"))
                 nc.tensor.matmul_mx(
-                    out=mask[m, u][:],
+                    out=mask[u][:],
                     lhsT=w2_mx[m][0][:].bitcast(FP8X4),
                     lhsT_scale=w2_mx[m][1][:],
-                    rhs=h_mx[u][0][:].bitcast(FP8X4),
-                    rhs_scale=h_mx[u][1][:],
+                    rhs=h_q[:, HALF * u : HALF * u + HALF].bitcast(FP8X4),
+                    rhs_scale=h_s[:, HALF * u : HALF * u + HALF],
                     start=True,
                     stop=True,
                 )
-        for m in range(2):
+            res = keep.tile([P, S], F32, name=f"res{m}")
             for u in range(2):
+                cols = slice(HALF * u, HALF * u + HALF)
                 prod = keep.tile([P, HALF], F32, name=f"prod{m}{u}")
                 nc.vector.scalar_tensor_tensor(
                     out=prod[:],
-                    in0=f_sb[u][:, m, :],
-                    scalar=mean_var[:, m, 0:1],
-                    in1=mask[m, u][:],
+                    in0=f_sb[:, m, cols],
+                    scalar=mean_var[m][:, 0:1],
+                    in1=mask[u][:],
                     op0=ALU.subtract,
                     op1=ALU.mult,
                 )
-                res = keep.tile([P, HALF], F32, name=f"res{m}{u}")
                 nc.scalar.activation(
-                    out=res[:], in_=prod[:], func=ACT.Relu, scale=rstd[:, m : m + 1], bias=bias_sb[:, m : m + 1]
+                    out=res[:, cols], in_=prod[:], func=ACT.Relu, scale=rstd[:], bias=bias_sb[:, m : m + 1]
                 )
-                nc.sync.dma_start(out=out[P * m : P * m + P, HALF * u : HALF * u + HALF], in_=res[:])
+                if m == 1:
+                    nc.sync.dma_start(out=out[P * m : P * m + P, cols], in_=res[:, cols])
+            if m == 0:
+                nc.sync.dma_start(out=out[P * m : P * m + P, :], in_=res[:])

from contextlib import ExitStack

import concourse.mybir as mybir

K, T, S, N, H = 512, 2048, 512, 256, 512
FLOPS = 2 * K * S * (H + N) + 2 * H * S * N

F32 = mybir.dt.float32
BF16 = mybir.dt.bfloat16
U32 = mybir.dt.uint32
I32 = mybir.dt.int32
U16 = mybir.dt.uint16
U8 = mybir.dt.uint8
FP8X4 = mybir.dt.float8_e4m3fn_x4
ACT = mybir.ActivationFunctionType
ALU = mybir.AluOpType

P = 128
PACK = 4
HALF = S // 2
CHUNK = 128
EPS = 0.05
W1_SCALAR = 80


def tile_picked_ymaskn_relu_p_kernel(
    tc, x_words, x_scales, e_words, e_scales, w1, w2, w3, bias, offs, fea, out
):
    nc = tc.nc
    with ExitStack() as ctx:
        keep = ctx.enter_context(tc.tile_pool(name="keep", bufs=1))
        psum = ctx.enter_context(tc.psum_pool(name="psum", bufs=1))

        x_list = keep.tile([P, S // 16], U16, name="x_list")
        e_list = keep.tile([P, S // 16], U16, name="e_list")
        x_scale_tab = keep.tile([P, T], U8, name="x_scale_tab", tag="x_scale_slot", align_bytes=64)
        e_scale_tab = keep.tile([P, T], U8, name="e_scale_tab", align_bytes=64)
        x_word_tab = keep.tile([P, T], U32, name="x_word_tab")
        e_word_tab = keep.tile([P, T], U32, name="e_word_tab", tag="e_word_slot", align_bytes=64)

        nc.vector.memset(x_scale_tab[:].bitcast(I32), 0)
        nc.vector.memset(e_scale_tab[:].bitcast(I32), 0)

        def load_scales(tab, scales, first):
            for r in range(4):
                nc.sync.dma_start(out=tab[first + r : P : 32, :].bitcast(I32), in_=scales[0, r:16:4, :].bitcast(I32))

        def load_words(tab, words):
            nc.sync.dma_start(out=tab[:].bitcast(I32), in_=words[0].rearrange("p n t -> p (n t)").bitcast(I32))

        def load_weight(w, name):
            raw = keep.tile([P, PACK, w.shape[1]], F32, name=name, tag=name)
            nc.sync.dma_start(out=raw[:], in_=w.rearrange("(p j) c -> p j c", j=PACK))
            return raw

        nc.sync.dma_start(x_list[:], offs)
        w1_raw = load_weight(w1, "w1_raw")
        load_scales(x_scale_tab, x_scales, 0)
        load_words(x_word_tab, x_words)
        nc.sync.dma_start(e_list[:], fea)
        load_scales(e_scale_tab, e_scales, 4)
        w3_raw = load_weight(w3, "w3_raw")
        load_words(e_word_tab, e_words)
        w2_raw = load_weight(w2, "w2_raw")
        bias_sb = keep.tile([P, 2], F32, name="bias_sb")
        with nc.allow_non_contiguous_dma(reason="one value a partition"):
            nc.sync.dma_start(out=bias_sb[:], in_=bias.rearrange("(m p) o -> p (m o)", p=P))
        one = keep.tile([P, 1], F32, name="one")
        nc.gpsimd.memset(one[:], 1.0)
        warm = keep.tile([P, 1], F32, name="warm")
        nc.scalar.activation(out=warm[:], in_=one[:], func=ACT.Abs_reciprocal_sqrt)

        w1_bf = keep.tile([P, H * PACK], BF16, name="w1_bf", align_bytes=64)
        w1_view = w1_bf[:].rearrange("p (t m j) -> p m t j", t=4, j=PACK)
        w1_src = w1_raw[:].rearrange("p j (m t) -> p m t j", t=4)
        nc.scalar.copy(out=w1_view[:, :W1_SCALAR], in_=w1_src[:, :W1_SCALAR])
        nc.vector.tensor_copy(out=w1_view[:, W1_SCALAR:], in_=w1_src[:, W1_SCALAR:])


        x_sc = keep.tile([P, S], U8, name="x_sc", align_bytes=64)
        e_sc = keep.tile([P, S], U8, name="e_sc", align_bytes=64)
        nc.vector.tensor_copy(x_sc[:], x_scale_tab[:].indirect(x_list[:]))

        w1_q = keep.tile([P, H], U32, name="w1_q", tag="x_scale_slot", align_bytes=64)
        w1_s = keep.tile([P, H], U8, name="w1_s", align_bytes=64)
        nc.vector.quantize_mx(out=w1_q[:].bitcast(FP8X4), scales=w1_s[:], in_=w1_bf[:])

        def gather_words(tab, lst, u, name):
            picked = keep.tile([P, HALF], U32, name=name, align_bytes=64)
            nc.vector.tensor_copy(picked[:], tab[:].indirect(lst[:, 16 * u : 16 * u + 16]))
            return picked

        x_w = [gather_words(x_word_tab, x_list, u, f"x_w{u}") for u in range(2)]
        nc.vector.tensor_copy(e_sc[:], e_scale_tab[:].indirect(e_list[:]))

        h_bf = keep.tile([P, S * PACK], BF16, name="h_bf", align_bytes=64)
        for c in range(4):
            u, j0 = c // 2, CHUNK * (c % 2)
            bank = psum.tile([P, 4, CHUNK], F32, name=f"h_bank{c}", tag=f"bank{c}")
            for t in range(4):
                nc.tensor.matmul_mx(
                    out=bank[:, t, :],
                    lhsT=w1_q[:, P * t : P * t + P].bitcast(FP8X4),
                    lhsT_scale=w1_s[:, P * t : P * t + P],
                    rhs=x_w[u][:, j0 : j0 + CHUNK].bitcast(FP8X4),
                    rhs_scale=x_sc[:, CHUNK * c : CHUNK * c + CHUNK],
                    start=True,
                    stop=True,
                )
            nc.scalar.activation(
                out=h_bf[:, PACK * CHUNK * c : PACK * CHUNK * (c + 1)].rearrange("p (j t) -> p j t", t=PACK),
                in_=bank[:].rearrange("p t j -> p j t"),
                func=ACT.Relu,
            )

        def weave(raw, bf, c0, width):
            src = raw[:, :, c0 : c0 + width].rearrange("p j (c i) -> p c j i", i=4)
            dst = bf[:].rearrange("p (c i j) -> p c j i", i=4, j=PACK)
            return dst, src

        def quantised(bf, name, tag):
            width = bf.shape[1] // PACK
            q = keep.tile([P, width], U32, name=name + "_q", tag=tag, align_bytes=64)
            s = keep.tile([P, width], U8, name=name + "_s", align_bytes=64)
            nc.vector.quantize_mx(out=q[:].bitcast(FP8X4), scales=s[:], in_=bf)
            return q, s

        w3_bf = keep.tile([P, N * PACK], BF16, name="w3_bf", align_bytes=64)
        nc.vector.tensor_copy(*weave(w3_raw, w3_bf, 0, N))
        w3_q, w3_s = quantised(w3_bf[:], "w3", "w3_q")

        e_w = [gather_words(e_word_tab, e_list, u, f"e_w{u}") for u in range(2)]
        h_q, h_s = quantised(h_bf[:], "h", "e_word_slot")
        f_bank = [psum.tile([P, S], F32, name=f"f_bank{m}") for m in range(2)]
        for u in range(2):
            for m in range(2):
                nc.tensor.matmul_mx(
                    out=f_bank[m][:, HALF * u : HALF * u + HALF],
                    lhsT=w3_q[:, P * m : P * m + P].bitcast(FP8X4),
                    lhsT_scale=w3_s[:, P * m : P * m + P],
                    rhs=e_w[u][:].bitcast(FP8X4),
                    rhs_scale=e_sc[4:P, HALF * u : HALF * u + HALF],
                    start=True,
                    stop=True,
                )

        w2_bf = [keep.tile([P, P * PACK], BF16, name=f"w2_bf{m}", tag=f"w2_slot{m}", align_bytes=64) for m in range(2)]
        for m in range(2):
            nc.scalar.copy(*weave(w2_raw, w2_bf[m], P * m, P))

        f_sb = keep.tile([P, 2, S], F32, name="f_sb", tag="w2_raw")
        w2_mx = [quantised(w2_bf[m][:], f"w2{m}", f"w2{m}_q") for m in range(2)]
        stats0 = keep.tile([P, 6], F32, name="stats0", tag="w2_slot0", align_bytes=64)
        nc.vector.bn_stats(out=stats0[:], in_=f_bank[0][:])
        nc.scalar.copy(out=f_sb[:, 0, :], in_=f_bank[0][:])
        mean_var0 = keep.tile([P, 2], F32, name="mean_var0")
        nc.vector.bn_aggr(out=mean_var0[:], in_=stats0[:])
        stats1 = keep.tile([P, 6], F32, name="stats1", tag="w2_slot1", align_bytes=64)
        nc.vector.bn_stats(out=stats1[:], in_=f_bank[1][:])
        nc.scalar.copy(out=f_sb[:, 1, :], in_=f_bank[1][:])
        mean_var1 = keep.tile([P, 2], F32, name="mean_var1")
        nc.vector.bn_aggr(out=mean_var1[:], in_=stats1[:])
        mean_var = [mean_var0, mean_var1]

        for m in range(2):
            rstd = keep.tile([P, 1], F32, name=f"rstd{m}")
            nc.scalar.activation(out=rstd[:], in_=mean_var[m][:, 1:2], func=ACT.Abs_reciprocal_sqrt, bias=EPS)
            mask = []
            for u in range(2):
                mask.append(psum.tile([P, HALF], F32, name=f"mask{m}{u}", tag=f"bank{2 * m + u}"))
                nc.tensor.matmul_mx(
                    out=mask[u][:],
                    lhsT=w2_mx[m][0][:].bitcast(FP8X4),
                    lhsT_scale=w2_mx[m][1][:],
                    rhs=h_q[:, HALF * u : HALF * u + HALF].bitcast(FP8X4),
                    rhs_scale=h_s[:, HALF * u : HALF * u + HALF],
                    start=True,
                    stop=True,
                )
            res = keep.tile([P, S], F32, name=f"res{m}")
            for u in range(2):
                cols = slice(HALF * u, HALF * u + HALF)
                prod = keep.tile([P, HALF], F32, name=f"prod{m}{u}")
                nc.vector.scalar_tensor_tensor(
                    out=prod[:],
                    in0=f_sb[:, m, cols],
                    scalar=mean_var[m][:, 0:1],
                    in1=mask[u][:],
                    op0=ALU.subtract,
                    op1=ALU.mult,
                )
                nc.scalar.activation(
                    out=res[:, cols], in_=prod[:], func=ACT.Relu, scale=rstd[:], bias=bias_sb[:, m : m + 1]
                )
                if m == 1:
                    nc.sync.dma_start(out=out[P * m : P * m + P, cols], in_=res[:, cols])
            if m == 0:
                nc.sync.dma_start(out=out[P * m : P * m + P, :], in_=res[:])
